import numpy as np
CORES = [36,164,52,180,100,228,116,244]
N = 8
T, EL, CAP, CAPP = 4096, 2, 1920, 512
E = N * EL
def entries(a): return a.T.reshape(-1)
def pack(v, P): return np.ascontiguousarray(np.asarray(v, np.int32).reshape(-1, P).T)
def lists(rng, how):
    if how == "uniform": return {"ex": np.stack([pack(rng.permutation(np.repeat(np.arange(E), CAPP))[:T], 16) for r in range(N)])}
    R = np.arange(N)[:, None]; c = rng.permutation(E); C = np.zeros((N, E), np.int64)
    if how == "bands":
        a = c % N; C = CAPP * ((R >= a) & (R <= a + CAP // CAPP)); C[a, np.arange(E)] = np.where(c < N, CAPP, rng.integers(1, CAPP + 1, E))
    if how == "full":
        g = T // CAPP; C[:, c[:g]] = CAPP; C[:, c[:g // 2]] = rng.integers(CAPP // 2, CAPP + 1, (N, g // 2))
    if how in ("skew", "sorted"):
        V = np.full((N, 3), CAP // N); V[:, 0] = rng.integers(2, CAP // N + 1, N); h = rng.integers(1, N - 2); V[h, 0] = 0; V[h + 1, 0] = 1; V[rng.integers(N), 1:] += CAP % N; V[rng.integers(N), 2] += 1
        W = rng.random((N, E)) ** 4 + 1e-9; W[:, c[:3]] = 0
        C = np.minimum(((T - T // 8 - V.sum(axis=1, keepdims=True)) * W / W.sum(axis=1, keepdims=True)).astype(np.int64), CAPP); C[:, c[:3]] = V
    if how == "thin":
        C = rng.integers(0, CAP // N + 1, (N, E)); C[1] = 1; C[[0, N // 2, N - 1]] = 0
    X = np.stack([rng.permutation(np.concatenate([np.repeat(np.arange(E), C[r]), np.full(T - C[r].sum(), -1)])) for r in range(N)])
    if how == "sorted": X = np.sort(X, axis=1); X[1::2] = X[1::2, ::-1].copy()
    return {"ex": np.stack([pack(v, 16) for v in X])}
def blank(d):
    for r in range(0, N, 2):
        u, i = np.unique(entries(d["ex"][r])[::-1], return_index=True); d["x"][r][:, T - 1 - i[u >= 0]] = 0
def setup_inputs(rng):
    return dict({"x": rng.standard_normal((N, 128, T), dtype=np.float32)}, **lists(rng, "uniform"))
def setup_inputs_bands(rng):
    d = setup_inputs(rng); d.update(lists(rng, "bands"))
    for k in ("x",): d[k] = (d[k].astype(np.float32) * 1048576.0).astype(d[k].dtype)
    blank(d)
    return d
def setup_inputs_full(rng):
    d = setup_inputs(rng); d.update(lists(rng, "full"))
    for k in ("x",): d[k] = (d[k].astype(np.float32) * (1 / 1024.0)).astype(d[k].dtype)
    blank(d)
    return d
def setup_inputs_skew(rng):
    d = setup_inputs(rng); d.update(lists(rng, "skew"))
    blank(d)
    return d
def setup_inputs_sorted(rng):
    d = setup_inputs(rng); d.update(lists(rng, "sorted"))
    blank(d)
    return d
def setup_inputs_thin(rng):
    d = setup_inputs(rng); d.update(lists(rng, "thin"))
    blank(d)
    return d
def check_inputs(x):
    bad = []
    if x["ex"].min() < -1 or x["ex"].max() >= E: bad.append("ex out of range")
    if max(int(np.bincount(entries(a)[entries(a) >= 0], minlength=E).max()) for a in x["ex"]) > CAPP: bad.append("more than CAPP tokens of one rank choose one expert")
    return bad
def reference(x, ex):
    X = np.concatenate(list(x), axis=1); e = np.concatenate([entries(a) for a in ex])
    k = np.nonzero(e >= 0)[0]; o = k[np.argsort(e[k], kind="stable")]; s = e[o]
    p = np.arange(len(o)) - np.searchsorted(s, s)
    Y = np.zeros((128, E * CAP), x.dtype); m = p < CAP; Y[:, CAP * s[m] + p[m]] = X[:, o[m]]
    return {"y": np.stack([Y[:, EL * CAP * r:EL * CAP * (r + 1)] for r in range(N)])}

@@ -1,0 +1,329 @@
+from concourse.bass import DstId, RemoteDMATransfer
+from concourse.mybir import AluOpType, ActivationFunctionType
+
+R_OFF, RR_OFF, A_OFF, AR_OFF = [1, 2, 3], [4], [5, 6], [7]
+NB = 5
+SLOT, BLK, ZERO = 512, 1024, 8192
+YSTEPS = [512, 1024, 1152, 1152]
+
+SCRATCH = {
+    "exi": ("sbuf", [128, 256], "int32"), "exb": ("sbuf", [128, 256], "bfloat16"),
+    "ones": ("sbuf", [128, 256], "bfloat16"), "nones": ("sbuf", [128, 128], "bfloat16"),
+    "zsel": ("sbuf", [128, 240], "bfloat16"), "upn": ("sbuf", [128, 128], "bfloat16"),
+    "idb": ("sbuf", [128, 128], "bfloat16"), "idh": ("sbuf", [128, 128], "float16"),
+    "hold": ("sbuf", [128, 512], "bfloat16"), "dsel": ("sbuf", [128, 256], "bfloat16"),
+    "va": ("sbuf", [128, 512], "bfloat16"), "vb": ("sbuf", [128, 512], "bfloat16"),
+    "dat": ("sbuf", [128, 512], "bfloat16"), "swr": ("sbuf", [128, 144], "bfloat16"),
+    "eq": ("sbuf", [128, 512], "bfloat16"), "cum": ("sbuf", [128, 512], "bfloat16"),
+    "mq": ("sbuf", [128, 512], "float16"),
+    "b0": ("sbuf", [128, 32], "float16"), "b1": ("sbuf", [128, 32], "float16"), "b2": ("sbuf", [128, 32], "float16"),
+    "neg": ("sbuf", [128, 32], "float32"),
+    "pidx": ("sbuf", [128, 8], "int32"), "pmod": ("sbuf", [128, 8], "int32"), "pcol": ("sbuf", [128, 8], "float32"),
+    "c16": ("sbuf", [128, 120], "float32"), "place": ("sbuf", [128, 120], "float32"),
+    "win": ("sbuf", [128, 8704], "bfloat16"),
+    "xs": ("sbuf", [128, 4096], "float32"), "sb": ("sbuf", [128, 4 * 1024], "float32"),
+    "rl": ("sbuf", [128, 1024], "float32"), "land": ("sbuf", [128, 8196], "float32"),
+    "yb": ("sbuf", [128, 3840], "float32"),
+    "meta": ("sbuf", [128, 48], "uint16"), "lst": ("sbuf", [128, 5 * 64], "uint16"),
+    "cin": ("sbuf", [128, 128], "uint16"),
+    "c8": ("sbuf", [128, 16], "float32"), "bp": ("sbuf", [128, 16], "float32"), "w8": ("sbuf", [128, 16], "float32"),
+    "th": ("sbuf", [128, 16 * 120], "float16"), "yo": ("sbuf", [128, 240], "float32"),
+    "ylst": ("sbuf", [128, 240], "uint16"),
+}
+for _i in range(8):
+    SCRATCH["p%d" % _i] = ("psum", [128, 512], "float32")
+
+SEMAPHORES = ["ex", "x0", "x1", "ones", "nones", "zb0", "zv", "zs", "zc", "c1", "hold", "swr", "dsel", "idb", "idh",
+              "zsel", "upn", "va", "vb", "pidx", "c16", "pmod", "pcol", "place", "exb", "ext", "datp", "dat",
+              "eqa", "eqb", "cuma", "cumb", "bs", "neg", "qa", "qb", "ma", "mb", "cntp", "cnt", "cself", "posp", "offs",
+              "sct", "c8", "bp", "w8", "tha", "thb", "yopa", "yopb", "yoa", "yob", "ylst", "st",
+              "sent", "metain", "xin", "rin", "cin", "din"]
+for _i in range(NB):
+    SEMAPHORES += ["lp%d" % _i, "lst%d" % _i, "gv%d" % _i, "gs%d" % _i]
+for _i in range(len(YSTEPS)):
+    SEMAPHORES += ["yv%d" % _i, "ys%d" % _i]
+
+COPY = ActivationFunctionType.Copy
+
+
+def ne(mask):
+    return bin(mask).count("1")
+
+
+def rank_program(g, core, T, topo):
+    S, n = T.sem, len(T.cores)
+    here = [c for c in T.cores if topo.host(c) == topo.host(core) and topo.chip(c) == topo.chip(core)]
+    if not here:
+        return
+    R = here[0]
+    rank = T.rank_of(R)
+    chipmates = [c for c in range(R - 8, R + 9) if c >= 0 and c != R and topo.host(c) == topo.host(R)
+                 and topo.chip(c) == topo.chip(R)]
+    RR = [c for c in chipmates if topo.die(c) == topo.die(R)][0]
+    A, AR = [c for c in chipmates if topo.die(c) != topo.die(R)][:2]
+    if core not in (R, RR, A, AR):
+        return
+    dests = lambda offs: [(rank + o) % n for o in offs]
+    far = T.cores[(rank + 1) % n]
+    off_mask = topo.mask(core, far)
+    near_mask = topo.mask(core, RR if core != RR else R)
+    push_mask = near_mask & ~off_mask
+    out = [0]
+
+    def send(dst, out_ap, in_ap, sem, mask):
+        rid, pid = topo.addr(dst, core)
+        g.remote_dma(out_ap, in_ap, S[sem], S.sent, pid, rid, mask)
+        out[0] += ne(mask)
+
+    def send_counts(ranks):
+        ids = []
+        for d in ranks:
+            rid, pid = topo.addr(T.cores[d], core)
+            ids.append(DstId(rid=rid, pnc=pid))
+        slot = T.cin[:, 16 * rank:16 * rank + 16]
+        g.remote_dma_fused([RemoteDMATransfer(dst_ids=ids, dma_engine_mask=off_mask, remote_sem=S.cin,
+                                              srcs=[T.meta[:, 32:48]], dsts=[slot] * len(ids))], local_sem=S.sent)
+        out[0] += ne(off_mask)
+
+    my_slot = T.land[:, BLK * rank:BLK * (rank + 1)]
+
+    if core in (RR, AR):
+        mine = dests(RR_OFF if core == RR else AR_OFF)
+        g.wait_ge(S.metain, ne(near_mask) if core == RR else ne(push_mask))
+        send_counts(dests(R_OFF) + mine if core == RR else mine)
+        g.wait_ge(S.rin, ne(push_mask))
+        send(T.cores[mine[0]], my_slot, T.rl[:], "din", off_mask)
+        g.wait_ge(S.sent, out[0])
+        return
+
+    isR = core == R
+    relay = RR if isR else AR
+    direct = dests(R_OFF if isR else A_OFF)
+    blocks = dests(RR_OFF if isR else AR_OFF) + direct + ([rank] if isR else [])
+    v, s, t, sy = g.vector, g.scalar, g.tensor, g.sync
+    winblk = lambda d: T.win[:, BLK * d:BLK * (d + 1)]
+
+    if isR:
+        sy.dma_start(T.exi[0:16, :], T.ex[:]).then_inc(S.ex, 16)
+        sy.dma_start(T.xs[:, 0:2048], T.x[:, 0:2048]).then_inc(S.x0, 16)
+        sy.dma_start(T.xs[:, 2048:4096], T.x[:, 2048:4096]).then_inc(S.x1, 16)
+
+    g.wait_ge(S.ones, 1)
+    if isR:
+        g.affine_select(T.zsel[0:16, :], T.ones[0:16, 0:240], [[1, 240]], AluOpType.is_equal, 0.0, -112, -1
+                        ).then_inc(S.zsel, 1)
+        g.iota(T.pidx[:, 0:1], [[0, 1]], 0, 1).then_inc(S.pidx, 1)
+    g.affine_select(T.idb[:], T.ones[:, 0:128], [[-1, 128]], AluOpType.is_equal, 0.0, 0, 1).then_inc(S.idb, 1)
+    if isR:
+        g.iota(T.c16[:], [[16, 120]], 0, 0, allow_small_or_imprecise_dtypes=True).then_inc(S.c16, 1)
+    g.iota(T.va[:], [[128, 32], [0, 16]], 0, 0, allow_small_or_imprecise_dtypes=True).then_inc(S.va, 1)
+    g.iota(T.vb[:], [[0, 32], [1, 16]], -1, 1, allow_small_or_imprecise_dtypes=True).then_inc(S.vb, 1)
+    if isR:
+        g.wait_ge(S.nones, 1)
+        g.affine_select(T.upn[:], T.nones[:], [[-1, 128]], AluOpType.is_ge, 0.0, 0, 1).then_inc(S.upn, 1)
+
+    v.memset(T.ones[:], 1.0).then_inc(S.ones, 1)
+    if isR:
+        v.memset(T.nones[:], -1.0).then_inc(S.nones, 1)
+    v.memset(winblk(blocks[0]), 0.0).then_inc(S.zb0, 1)
+    v.memset(T.swr[:], 0.0).then_inc(S.c1, 1)
+    v.memset(T.dsel[:], 0.0).then_inc(S.c1, 1)
+    nc1 = 2
+    if isR:
+        v.memset(T.hold[:], 1.0).then_inc(S.c1, 1)
+        nc1 = 3
+    v.memset(winblk(blocks[1]), 0.0).then_inc(S.zv, 1)
+    v.memset(winblk(blocks[2]), 0.0).then_inc(S.zv, 1)
+    v.wait_ge(S.c1, nc1)
+    v.memset(T.swr[:, 15::16], 1.0).then_inc(S.swr, 1)
+    if isR:
+        v.memset(T.hold[:, 0::32], 0.0).then_inc(S.hold, 1)
+        v.memset(T.land[:, ZERO:ZERO + 4], 0.0).then_inc(S.zc, 1)
+        v.wait_ge(S.pidx, 1)
+        v.tensor_scalar(T.pmod[:, 0:1], T.pidx[:, 0:1], 15, None, AluOpType.bitwise_and).then_inc(S.pmod, 1)
+    v.wait_ge(S.idb, 1)
+    v.tensor_copy(T.dsel[:, 0:128:16], T.idb[:, 0:128:16]).then_inc(S.dsel, 1)
+    v.tensor_copy(T.dsel[:, 129:256:16], T.idb[:, 1:128:16]).then_inc(S.dsel, 1)
+    if isR:
+        v.tensor_copy(T.idh[:], T.idb[:]).then_inc(S.idh, 1)
+        v.wait_ge(S.pmod, 1)
+        v.tensor_copy(T.pcol[:, 0:1], T.pmod[:, 0:1]).then_inc(S.pcol, 1)
+        v.wait_ge(S.ex, 16)
+        v.tensor_copy(T.exb[0:16, :], T.exi[0:16, :]).then_inc(S.exb, 1)
+        v.wait_ge(S.pcol, 1)
+        v.wait_ge(S.c16, 1)
+        v.tensor_scalar(T.place[:], T.c16[:], T.pcol[:, 0:1], None, AluOpType.add).then_inc(S.place, 1)
+
+    s.wait_ge(S.zb0, 1)
+    nzs = 0
+    for d in blocks[3:]:
+        s.activation(winblk(d), winblk(blocks[0]), COPY).then_inc(S.zs, 1)
+        nzs += 1
+
+    if isR:
+        EXT = T.p0[:, 0:32]
+        t.wait_ge(S.exb, 1)
+        t.wait_ge(S.zsel, 1)
+        for h in range(8):
+            mm = t.matmul(EXT, T.zsel[0:16, 112 - 16 * h:240 - 16 * h], T.exb[0:16, h::8], h == 0, h == 7)
+        mm.then_inc(S.ext, 1)
+    t.wait_ge(S.va, 1)
+    t.wait_ge(S.vb, 1)
+    t.wait_ge(S.dsel, 2)
+    t.matmul(T.p4[:], T.dsel[:, 0:128], T.va[:], True, False)
+    t.matmul(T.p4[:], T.dsel[:, 128:256], T.vb[:], False, True).then_inc(S.datp, 1)
+    s.wait_ge(S.datp, 1)
+    s.activation(T.dat[:], T.p4[:], COPY).then_inc(S.dat, 1)
+    if isR:
+        v.wait_ge(S.ext, 1)
+        halves = (("a", 0, T.p1), ("b", 256, T.p6))
+        for tag, o, _ in halves:
+            for k in range(8):
+                v.tensor_scalar(T.eq[:, o + 32 * k:o + 32 * k + 32], EXT, float(o // 32 + k), None, AluOpType.is_equal
+                                ).then_inc(S["eq" + tag], 1)
+            v.wait_ge(S["eq" + tag], 8)
+            if tag == "a":
+                v.wait_ge(S.hold, 1)
+            v.tensor_tensor_scan(T.cum[:, o:o + 256], T.hold[:, o:o + 256], T.eq[:, o:o + 256], 0.0, AluOpType.mult,
+                                 AluOpType.add).then_inc(S["cum" + tag], 1)
+        v.tensor_scalar(T.neg[:], EXT, 0.0, None, AluOpType.is_lt).then_inc(S.neg, 1)
+        v.tensor_scalar(T.b0[:], EXT, 512.0, None, AluOpType.mult).then_inc(S.bs, 1)
+        v.tensor_scalar(T.b1[:], EXT, 0.0, 8704.0, AluOpType.is_lt, AluOpType.mult).then_inc(S.bs, 1)
+        v.wait_ge(S.neg, 1)
+        v.wait_ge(S.place, 1)
+        v.tensor_tensor(T.b2[:], T.neg[:], T.place[:, 0:32], AluOpType.mult).then_inc(S.bs, 1)
+
+        t.wait_ge(S.upn, 1)
+        t.wait_ge(S.ones, 1)
+        for tag, o, P in halves:
+            t.wait_ge(S["cum" + tag], 1)
+            t.matmul(P[:, 0:256], T.ones[:, 0:128], T.cum[:, o:o + 256], True, False)
+            t.matmul(P[:, 0:256], T.upn[:], T.eq[:, o:o + 256], False, True).then_inc(S["q" + tag], 1)
+            v.wait_ge(S["q" + tag], 1)
+            v.tensor_tensor(T.mq[:, o:o + 256], P[:, 0:256], T.eq[:, o:o + 256], AluOpType.mult
+                            ).then_inc(S["m" + tag], 1)
+        t.matmul(T.p2[:, 0:16], T.ones[:, 0:128], T.cum[:, 31::32], True, True).then_inc(S.cntp, 1)
+        v.wait_ge(S.cntp, 1)
+        v.tensor_copy(T.meta[:, 32:48], T.p2[:, 0:16]).then_inc(S.cnt, 1)
+        v.tensor_copy(T.cin[:, 16 * rank:16 * rank + 16], T.p2[:, 0:16]).then_inc(S.cself, 1)
+        t.wait_ge(S.idh, 1)
+        t.wait_ge(S.bs, 3)
+        pos = T.p3[:, 0:32]
+        for i, b in enumerate((T.b0, T.b1, T.b2)):
+            t.matmul(pos, T.idh[:], b[:], i == 0, False)
+        for k in range(16):
+            if k % 8 == 0:
+                t.wait_ge(S["ma" if k == 0 else "mb"], 1)
+            mm = t.matmul(pos, T.idh[:], T.mq[:, 32 * k:32 * k + 32], False, k == 15)
+        mm.then_inc(S.posp, 1)
+        v.wait_ge(S.posp, 1)
+        v.tensor_copy(T.meta[:, 0:32], pos).then_inc(S.offs, 1)
+        v.wait_ge(S.offs, 1)
+    else:
+        v.wait_ge(S.metain, ne(near_mask))
+
+    v.wait_ge(S.dat, 1)
+    v.wait_ge(S.zb0, 1)
+    v.wait_ge(S.zv, 2)
+    if nzs:
+        v.wait_ge(S.zs, nzs)
+    v.tensor_copy(T.win[:].indirect(T.meta[:, 0:32]), T.dat[:]).then_inc(S.sct, 1)
+    t.wait_ge(S.swr, 1)
+    t.wait_ge(S.sct, 1)
+    banks = [T.p5, T.p7, T.p4, T.p0, T.p1]
+    for i, d in enumerate(blocks):
+        L = banks[i][:, 0:64]
+        for c in range(16):
+            mm = t.matmul(L, T.swr[:, 15 - c:143 - c], T.win[:, BLK * d + c:BLK * (d + 1):16], c == 0, c == 15)
+        mm.then_inc(S["lp%d" % i], 1)
+        v.wait_ge(S["lp%d" % i], 1)
+        v.tensor_copy(T.lst[:, 64 * i:64 * i + 64], L).then_inc(S["lst%d" % i], 1)
+        dst, o = (T.land, BLK * rank) if d == rank else (T.sb, BLK * i)
+        for q in (v, s):
+            q.wait_ge(S["lst%d" % i], 1)
+            if i == 0:
+                if isR:
+                    q.wait_ge(S.x0, 16)
+                    q.wait_ge(S.x1, 16)
+                else:
+                    q.wait_ge(S.xin, 2 * ne(near_mask))
+        v.tensor_copy(dst[:, o:o + SLOT], T.xs[:].indirect(T.lst[:, 64 * i:64 * i + 32])).then_inc(S["gv%d" % i], 1)
+        s.activation(dst[:, o + SLOT:o + BLK], T.xs[:].indirect(T.lst[:, 64 * i + 32:64 * i + 64]), COPY
+                     ).then_inc(S["gs%d" % i], 1)
+
+    if isR:
+        g.wait_ge(S.x0, 16)
+        send(A, T.xs[:, 0:2048], T.xs[:, 0:2048], "xin", near_mask)
+        g.wait_ge(S.cnt, 1)
+        send(RR, T.meta[:, 32:48], T.meta[:, 32:48], "metain", near_mask)
+        g.wait_ge(S.offs, 1)
+        send(A, T.meta[:], T.meta[:], "metain", near_mask)
+        g.wait_ge(S.x1, 16)
+        send(A, T.xs[:, 2048:4096], T.xs[:, 2048:4096], "xin", near_mask)
+    else:
+        g.wait_ge(S.metain, ne(near_mask))
+        send_counts(direct)
+        send(AR, T.meta[:, 32:48], T.meta[:, 32:48], "metain", push_mask)
+    for i, d in enumerate(blocks):
+        if d == rank:
+            continue
+        g.wait_ge(S["gv%d" % i], 1)
+        g.wait_ge(S["gs%d" % i], 1)
+        src = T.sb[:, BLK * i:BLK * (i + 1)]
+        if i == 0:
+            send(relay, T.rl[:], src, "rin", push_mask)
+        else:
+            send(T.cores[d], my_slot, src, "din", off_mask)
+    g.wait_ge(S.sent, out[0])
+    if not isR:
+        return
+
+    v.wait_ge(S.cself, 1)
+    v.wait_ge(S.cin, (n - 1) * ne(off_mask))
+    for e in range(2):
+        v.tensor_copy(T.c8[:, 8 * e:8 * e + 8], T.cin[:, 2 * rank + e::16]).then_inc(S.c8, 1)
+    v.wait_ge(S.c8, 2)
+    for e in range(2):
+        c = T.c8[:, 8 * e:8 * e + 8]
+        v.tensor_tensor_scan(T.bp[:, 8 * e:8 * e + 8], T.ones[:, 0:8], c, 0.0, AluOpType.mult, AluOpType.add
+                             ).then_inc(S.bp, 1)
+        v.tensor_scalar(T.w8[:, 8 * e:8 * e + 8], c, -1.0, float(BLK), AluOpType.mult, AluOpType.add
+                        ).then_inc(S.w8, 1)
+    v.wait_ge(S.bp, 2)
+    v.wait_ge(S.w8, 2)
+    for e, tag, P in ((0, "a", T.p3), (1, "b", T.p6)):
+        for r in range(n):
+            j = 8 * e + r
+            v.tensor_scalar(T.th[:, 120 * j:120 * j + 120], T.place[:], T.bp[:, j:j + 1], T.w8[:, j:j + 1],
+                            AluOpType.is_ge, AluOpType.mult).then_inc(S["th" + tag], 1)
+        t.wait_ge(S["th" + tag], n)
+        for r in range(n):
+            j = 8 * e + r
+            mm = t.matmul(P[:, 0:120], T.idh[:], T.th[:, 120 * j:120 * j + 120], r == 0, r == n - 1)
+        mm.then_inc(S["yop" + tag], 1)
+    for e, tag, P in ((0, "a", T.p3), (1, "b", T.p6)):
+        o = T.yo[:, 120 * e:120 * e + 120]
+        v.wait_ge(S["yop" + tag], 1)
+        v.tensor_tensor(o, P[:, 0:120], T.place[:], AluOpType.add).then_inc(S["yo" + tag], 1)
+        v.wait_ge(S["yo" + tag], 1)
+        v.tensor_scalar(T.ylst[:, 120 * e:120 * e + 120], o, float(SLOT * e), float(ZERO), AluOpType.add,
+                        AluOpType.min).then_inc(S.ylst, 1)
+
+    last = len(blocks) - 1
+    for q in (v, s):
+        q.wait_ge(S.ylst, 2)
+        q.wait_ge(S.zc, 1)
+        q.wait_ge(S["gv%d" % last], 1)
+        q.wait_ge(S["gs%d" % last], 1)
+        q.wait_ge(S.din, (n - 1) * ne(off_mask))
+    o = 0
+    for i, w in enumerate(YSTEPS):
+        m = o + w // 2
+        W = T.land[:, 0:ZERO + 1]
+        v.tensor_copy(T.yb[:, o:m], W.indirect(T.ylst[:, o // 16:m // 16])).then_inc(S["yv%d" % i], 1)
+        s.activation(T.yb[:, m:o + w], W.indirect(T.ylst[:, m // 16:(o + w) // 16]), COPY).then_inc(S["ys%d" % i], 1)
+        sy.wait_ge(S["yv%d" % i], 1)
+        sy.wait_ge(S["ys%d" % i], 1)
+        sy.dma_start(T.y[:, o:o + w], T.yb[:, o:o + w]).then_inc(S.st, 16)
+        o += w
+    sy.wait_ge(S.st, 16 * len(YSTEPS))

@@ -1,10 +1,13 @@
 from concourse.bass import DstId, RemoteDMATransfer
 from concourse.mybir import AluOpType, ActivationFunctionType
 
-R_OFF, RR_OFF, A_OFF, AR_OFF = [1, 2, 3], [4], [5, 6], [7]
-NB = 5
-SLOT, BLK, ZERO = 512, 1024, 8192
-YSTEPS = [512, 1024, 1152, 1152]
+R_UNITS = [("d", 1, 0), (0, 4, 0), ("d", 2, 0), ("d", 3, 0), (0, 4, 1), (1, 3, 1), (2, 2, 1), ("d", 1, 1)]
+A_UNITS = [("d", 7, 0), ("d", 5, 0), (0, 7, 1), (1, 6, 1), ("d", 6, 0), ("d", 5, 1)]
+R_COUNTS = {0: [4, 1], 1: [3], 2: [2]}
+A_COUNTS = {"d": [5], 0: [7], 1: [6]}
+NB, NU = 5, 9
+SLOT, BLK, ZERO = 512, 1024, 4096
+YSTEPS = [(0, 640), (0, 1280), (1, 512), (1, 640), (1, 768)]
 
 SCRATCH = {
     "exi": ("sbuf", [128, 256], "int32"), "exb": ("sbuf", [128, 256], "bfloat16"),
@@ -21,8 +24,9 @@ SCRATCH = {
     "pidx": ("sbuf", [128, 8], "int32"), "pmod": ("sbuf", [128, 8], "int32"), "pcol": ("sbuf", [128, 8], "float32"),
     "c16": ("sbuf", [128, 120], "float32"), "place": ("sbuf", [128, 120], "float32"),
     "win": ("sbuf", [128, 8704], "bfloat16"),
-    "xs": ("sbuf", [128, 4096], "float32"), "sb": ("sbuf", [128, 4 * 1024], "float32"),
-    "rl": ("sbuf", [128, 1024], "float32"), "land": ("sbuf", [128, 8196], "float32"),
+    "xs": ("sbuf", [128, 4096], "float32"), "sb": ("sbuf", [128, 8 * 512], "float32"),
+    "rl": ("sbuf", [128, 1024], "float32"),
+    "land0": ("sbuf", [128, 4100], "float32"), "land1": ("sbuf", [128, 4100], "float32"),
     "yb": ("sbuf", [128, 3840], "float32"),
     "meta": ("sbuf", [128, 48], "uint16"), "lst": ("sbuf", [128, 5 * 64], "uint16"),
     "cin": ("sbuf", [128, 128], "uint16"),
@@ -37,9 +41,11 @@ SEMAPHORES = ["ex", "x0", "x1", "ones", "nones", "zb0", "zv", "zs", "zc", "c1", 
               "zsel", "upn", "va", "vb", "pidx", "c16", "pmod", "pcol", "place", "exb", "ext", "datp", "dat",
               "eqa", "eqb", "cuma", "cumb", "bs", "neg", "qa", "qb", "ma", "mb", "cntp", "cnt", "cself", "posp", "offs",
               "sct", "c8", "bp", "w8", "tha", "thb", "yopa", "yopb", "yoa", "yob", "ylst", "st",
-              "sent", "metain", "xin", "rin", "cin", "din"]
+              "sent", "metain", "xin", "rin0", "rin1", "cin", "din0", "din1"]
 for _i in range(NB):
-    SEMAPHORES += ["lp%d" % _i, "lst%d" % _i, "gv%d" % _i, "gs%d" % _i]
+    SEMAPHORES += ["lp%d" % _i, "lst%d" % _i]
+for _i in range(NU):
+    SEMAPHORES += ["gv%d" % _i, "gs%d" % _i]
 for _i in range(len(YSTEPS)):
     SEMAPHORES += ["yv%d" % _i, "ys%d" % _i]
 
@@ -59,14 +65,15 @@ def rank_program(g, core, T, topo):
     rank = T.rank_of(R)
     chipmates = [c for c in range(R - 8, R + 9) if c >= 0 and c != R and topo.host(c) == topo.host(R)
                  and topo.chip(c) == topo.chip(R)]
-    RR = [c for c in chipmates if topo.die(c) == topo.die(R)][0]
-    A, AR = [c for c in chipmates if topo.die(c) != topo.die(R)][:2]
-    if core not in (R, RR, A, AR):
+    RR = [c for c in chipmates if topo.die(c) == topo.die(R)][:len(R_COUNTS)]
+    other = [c for c in chipmates if topo.die(c) != topo.die(R)]
+    A, AR = other[0], other[1:len(A_COUNTS)]
+    if core != R and core != A and core not in RR and core not in AR:
         return
-    dests = lambda offs: [(rank + o) % n for o in offs]
-    far = T.cores[(rank + 1) % n]
+    rk = lambda o: (rank + o) % n
+    far = T.cores[rk(1)]
     off_mask = topo.mask(core, far)
-    near_mask = topo.mask(core, RR if core != RR else R)
+    near_mask = topo.mask(core, R if core != R else A)
     push_mask = near_mask & ~off_mask
     out = [0]
 
@@ -75,31 +82,40 @@ def rank_program(g, core, T, topo):
         g.remote_dma(out_ap, in_ap, S[sem], S.sent, pid, rid, mask)
         out[0] += ne(mask)
 
-    def send_counts(ranks):
+    def send_counts(dsts, slot, sem, mask):
         ids = []
-        for d in ranks:
-            rid, pid = topo.addr(T.cores[d], core)
+        for d in dsts:
+            rid, pid = topo.addr(d, core)
             ids.append(DstId(rid=rid, pnc=pid))
-        slot = T.cin[:, 16 * rank:16 * rank + 16]
-        g.remote_dma_fused([RemoteDMATransfer(dst_ids=ids, dma_engine_mask=off_mask, remote_sem=S.cin,
+        g.remote_dma_fused([RemoteDMATransfer(dst_ids=ids, dma_engine_mask=mask, remote_sem=S[sem],
                                               srcs=[T.meta[:, 32:48]], dsts=[slot] * len(ids))], local_sem=S.sent)
-        out[0] += ne(off_mask)
+        out[0] += ne(mask)
 
-    my_slot = T.land[:, BLK * rank:BLK * (rank + 1)]
+    land = (T.land0, T.land1)
+    cslot = T.cin[:, 16 * rank:16 * rank + 16]
+    my_slot = lambda e: land[e][:, SLOT * rank:SLOT * (rank + 1)]
 
-    if core in (RR, AR):
-        mine = dests(RR_OFF if core == RR else AR_OFF)
-        g.wait_ge(S.metain, ne(near_mask) if core == RR else ne(push_mask))
-        send_counts(dests(R_OFF) + mine if core == RR else mine)
-        g.wait_ge(S.rin, ne(push_mask))
-        send(T.cores[mine[0]], my_slot, T.rl[:], "din", off_mask)
+    if core in RR or core in AR:
+        onR = core in RR
+        me = (RR if onR else AR).index(core)
+        counts, units = (R_COUNTS, R_UNITS) if onR else (A_COUNTS, A_UNITS)
+        g.wait_ge(S.metain, ne(near_mask) if onR else ne(push_mask))
+        send_counts([T.cores[rk(o)] for o in counts[me]], cslot, "cin", off_mask)
+        for j, (_, o, e) in enumerate([u for u in units if u[0] == me]):
+            g.wait_ge(S["rin%d" % j], ne(push_mask))
+            send(T.cores[rk(o)], my_slot(e), T.rl[:, SLOT * j:SLOT * (j + 1)], "din%d" % e, off_mask)
         g.wait_ge(S.sent, out[0])
         return
 
     isR = core == R
-    relay = RR if isR else AR
-    direct = dests(R_OFF if isR else A_OFF)
-    blocks = dests(RR_OFF if isR else AR_OFF) + direct + ([rank] if isR else [])
+    relays = RR if isR else AR
+    units = [(w, rk(o), e) for w, o, e in (R_UNITS if isR else A_UNITS)]
+    blocks = []
+    for _, d, _ in units:
+        if d not in blocks:
+            blocks.append(d)
+    if isR:
+        blocks.append(rank)
     v, s, t, sy = g.vector, g.scalar, g.tensor, g.sync
     winblk = lambda d: T.win[:, BLK * d:BLK * (d + 1)]
 
@@ -138,7 +154,8 @@ def rank_program(g, core, T, topo):
     v.memset(T.swr[:, 15::16], 1.0).then_inc(S.swr, 1)
     if isR:
         v.memset(T.hold[:, 0::32], 0.0).then_inc(S.hold, 1)
-        v.memset(T.land[:, ZERO:ZERO + 4], 0.0).then_inc(S.zc, 1)
+        for e in range(2):
+            v.memset(land[e][:, ZERO:ZERO + 4], 0.0).then_inc(S.zc, 1)
         v.wait_ge(S.pidx, 1)
         v.tensor_scalar(T.pmod[:, 0:1], T.pidx[:, 0:1], 15, None, AluOpType.bitwise_and).then_inc(S.pmod, 1)
     v.wait_ge(S.idb, 1)
@@ -205,7 +222,7 @@ def rank_program(g, core, T, topo):
         t.matmul(T.p2[:, 0:16], T.ones[:, 0:128], T.cum[:, 31::32], True, True).then_inc(S.cntp, 1)
         v.wait_ge(S.cntp, 1)
         v.tensor_copy(T.meta[:, 32:48], T.p2[:, 0:16]).then_inc(S.cnt, 1)
-        v.tensor_copy(T.cin[:, 16 * rank:16 * rank + 16], T.p2[:, 0:16]).then_inc(S.cself, 1)
+        v.tensor_copy(cslot, T.p2[:, 0:16]).then_inc(S.cself, 1)
         t.wait_ge(S.idh, 1)
         t.wait_ge(S.bs, 3)
         pos = T.p3[:, 0:32]
@@ -232,48 +249,62 @@ def rank_program(g, core, T, topo):
     t.wait_ge(S.sct, 1)
     banks = [T.p5, T.p7, T.p4, T.p0, T.p1]
     for i, d in enumerate(blocks):
-        L = banks[i][:, 0:64]
         for c in range(16):
-            mm = t.matmul(L, T.swr[:, 15 - c:143 - c], T.win[:, BLK * d + c:BLK * (d + 1):16], c == 0, c == 15)
+            mm = t.matmul(banks[i][:, 0:64], T.swr[:, 15 - c:143 - c], T.win[:, BLK * d + c:BLK * (d + 1):16],
+                          c == 0, c == 15)
         mm.then_inc(S["lp%d" % i], 1)
-        v.wait_ge(S["lp%d" % i], 1)
-        v.tensor_copy(T.lst[:, 64 * i:64 * i + 64], L).then_inc(S["lst%d" % i], 1)
-        dst, o = (T.land, BLK * rank) if d == rank else (T.sb, BLK * i)
-        for q in (v, s):
-            q.wait_ge(S["lst%d" % i], 1)
-            if i == 0:
-                if isR:
-                    q.wait_ge(S.x0, 16)
-                    q.wait_ge(S.x1, 16)
-                else:
-                    q.wait_ge(S.xin, 2 * ne(near_mask))
-        v.tensor_copy(dst[:, o:o + SLOT], T.xs[:].indirect(T.lst[:, 64 * i:64 * i + 32])).then_inc(S["gv%d" % i], 1)
-        s.activation(dst[:, o + SLOT:o + BLK], T.xs[:].indirect(T.lst[:, 64 * i + 32:64 * i + 64]), COPY
-                     ).then_inc(S["gs%d" % i], 1)
+    for q in (v, s):
+        if isR:
+            q.wait_ge(S.x0, 16)
+            q.wait_ge(S.x1, 16)
+        else:
+            q.wait_ge(S.xin, 2 * ne(near_mask))
+    listed = []
+
+    def need_list(d):
+        i = blocks.index(d)
+        if i not in listed:
+            listed.append(i)
+            v.wait_ge(S["lp%d" % i], 1)
+            v.tensor_copy(T.lst[:, 64 * i:64 * i + 64], banks[i][:, 0:64]).then_inc(S["lst%d" % i], 1)
+            for q in (v, s):
+                q.wait_ge(S["lst%d" % i], 1)
+        return 64 * i
+
+    for u, (_, d, e) in enumerate(units):
+        c, o, h = need_list(d) + 32 * e, SLOT * u, SLOT // 2
+        v.tensor_copy(T.sb[:, o:o + h], T.xs[:].indirect(T.lst[:, c:c + 16])).then_inc(S["gv%d" % u], 1)
+        s.activation(T.sb[:, o + h:o + SLOT], T.xs[:].indirect(T.lst[:, c + 16:c + 32]), COPY
+                     ).then_inc(S["gs%d" % u], 1)
+    if isR:
+        c, u = need_list(rank), len(units)
+        v.tensor_copy(my_slot(0), T.xs[:].indirect(T.lst[:, c:c + 32])).then_inc(S["gv%d" % u], 1)
+        s.activation(my_slot(1), T.xs[:].indirect(T.lst[:, c + 32:c + 64]), COPY).then_inc(S["gs%d" % u], 1)
 
     if isR:
         g.wait_ge(S.x0, 16)
         send(A, T.xs[:, 0:2048], T.xs[:, 0:2048], "xin", near_mask)
         g.wait_ge(S.cnt, 1)
-        send(RR, T.meta[:, 32:48], T.meta[:, 32:48], "metain", near_mask)
+        send_counts(RR, T.meta[:, 32:48], "metain", near_mask)
         g.wait_ge(S.offs, 1)
         send(A, T.meta[:], T.meta[:], "metain", near_mask)
         g.wait_ge(S.x1, 16)
         send(A, T.xs[:, 2048:4096], T.xs[:, 2048:4096], "xin", near_mask)
     else:
         g.wait_ge(S.metain, ne(near_mask))
-        send_counts(direct)
-        send(AR, T.meta[:, 32:48], T.meta[:, 32:48], "metain", push_mask)
-    for i, d in enumerate(blocks):
-        if d == rank:
-            continue
-        g.wait_ge(S["gv%d" % i], 1)
-        g.wait_ge(S["gs%d" % i], 1)
-        src = T.sb[:, BLK * i:BLK * (i + 1)]
-        if i == 0:
-            send(relay, T.rl[:], src, "rin", push_mask)
+        send_counts([T.cores[rk(o)] for o in A_COUNTS["d"]], cslot, "cin", off_mask)
+        send_counts(AR, T.meta[:, 32:48], "metain", push_mask)
+    pushed = [0] * len(relays)
+    for u, (w, d, e) in enumerate(units):
+        g.wait_ge(S["gv%d" % u], 1)
+        g.wait_ge(S["gs%d" % u], 1)
+        src = T.sb[:, SLOT * u:SLOT * (u + 1)]
+        if w == "d":
+            send(T.cores[d], my_slot(e), src, "din%d" % e, off_mask)
         else:
-            send(T.cores[d], my_slot, src, "din", off_mask)
+            j = pushed[w]
+            pushed[w] += 1
+            send(relays[w], T.rl[:, SLOT * j:SLOT * (j + 1)], src, "rin%d" % j, push_mask)
     g.wait_ge(S.sent, out[0])
     if not isR:
         return
@@ -287,7 +318,7 @@ def rank_program(g, core, T, topo):
         c = T.c8[:, 8 * e:8 * e + 8]
         v.tensor_tensor_scan(T.bp[:, 8 * e:8 * e + 8], T.ones[:, 0:8], c, 0.0, AluOpType.mult, AluOpType.add
                              ).then_inc(S.bp, 1)
-        v.tensor_scalar(T.w8[:, 8 * e:8 * e + 8], c, -1.0, float(BLK), AluOpType.mult, AluOpType.add
+        v.tensor_scalar(T.w8[:, 8 * e:8 * e + 8], c, -1.0, float(SLOT), AluOpType.mult, AluOpType.add
                         ).then_inc(S.w8, 1)
     v.wait_ge(S.bp, 2)
     v.wait_ge(S.w8, 2)
@@ -306,20 +337,21 @@ def rank_program(g, core, T, topo):
         v.wait_ge(S["yop" + tag], 1)
         v.tensor_tensor(o, P[:, 0:120], T.place[:], AluOpType.add).then_inc(S["yo" + tag], 1)
         v.wait_ge(S["yo" + tag], 1)
-        v.tensor_scalar(T.ylst[:, 120 * e:120 * e + 120], o, float(SLOT * e), float(ZERO), AluOpType.add,
-                        AluOpType.min).then_inc(S.ylst, 1)
+        v.tensor_scalar(T.ylst[:, 120 * e:120 * e + 120], o, float(ZERO), None, AluOpType.min).then_inc(S.ylst, 1)
 
-    last = len(blocks) - 1
+    last = len(units)
     for q in (v, s):
         q.wait_ge(S.ylst, 2)
-        q.wait_ge(S.zc, 1)
+        q.wait_ge(S.zc, 2)
         q.wait_ge(S["gv%d" % last], 1)
         q.wait_ge(S["gs%d" % last], 1)
-        q.wait_ge(S.din, (n - 1) * ne(off_mask))
     o = 0
-    for i, w in enumerate(YSTEPS):
+    for i, (e, w) in enumerate(YSTEPS):
+        if i == 0 or YSTEPS[i - 1][0] != e:
+            for q in (v, s):
+                q.wait_ge(S["din%d" % e], (n - 1) * ne(off_mask))
         m = o + w // 2
-        W = T.land[:, 0:ZERO + 1]
+        W = land[e][:, 0:ZERO + 1]
         v.tensor_copy(T.yb[:, o:m], W.indirect(T.ylst[:, o // 16:m // 16])).then_inc(S["yv%d" % i], 1)
         s.activation(T.yb[:, m:o + w], W.indirect(T.ylst[:, m // 16:(o + w) // 16]), COPY).then_inc(S["ys%d" % i], 1)
         sy.wait_ge(S["yv%d" % i], 1)

from concourse.bass import DstId, RemoteDMATransfer
from concourse.mybir import AluOpType, ActivationFunctionType

R_UNITS = [("d", 1, 0), (0, 4, 0), ("d", 2, 0), ("d", 3, 0), (0, 4, 1), (1, 3, 1), (2, 2, 1), ("d", 1, 1)]
A_UNITS = [("d", 7, 0), ("d", 5, 0), (0, 7, 1), (1, 6, 1), ("d", 6, 0), ("d", 5, 1)]
R_COUNTS = {0: [4, 1], 1: [3], 2: [2]}
A_COUNTS = {"d": [5], 0: [7], 1: [6]}
NB, NU = 5, 9
SLOT, BLK, ZERO = 512, 1024, 4096
YSTEPS = [(0, 640), (0, 1280), (1, 512), (1, 640), (1, 768)]

SCRATCH = {
    "exi": ("sbuf", [128, 256], "int32"), "exb": ("sbuf", [128, 256], "bfloat16"),
    "ones": ("sbuf", [128, 256], "bfloat16"), "nones": ("sbuf", [128, 128], "bfloat16"),
    "zsel": ("sbuf", [128, 240], "bfloat16"), "upn": ("sbuf", [128, 128], "bfloat16"),
    "idb": ("sbuf", [128, 128], "bfloat16"), "idh": ("sbuf", [128, 128], "float16"),
    "hold": ("sbuf", [128, 512], "bfloat16"), "dsel": ("sbuf", [128, 256], "bfloat16"),
    "va": ("sbuf", [128, 512], "bfloat16"), "vb": ("sbuf", [128, 512], "bfloat16"),
    "dat": ("sbuf", [128, 512], "bfloat16"), "swr": ("sbuf", [128, 144], "bfloat16"),
    "eq": ("sbuf", [128, 512], "bfloat16"), "cum": ("sbuf", [128, 512], "bfloat16"),
    "mq": ("sbuf", [128, 512], "float16"),
    "b0": ("sbuf", [128, 32], "float16"), "b1": ("sbuf", [128, 32], "float16"), "b2": ("sbuf", [128, 32], "float16"),
    "neg": ("sbuf", [128, 32], "float32"),
    "pidx": ("sbuf", [128, 8], "int32"), "pmod": ("sbuf", [128, 8], "int32"), "pcol": ("sbuf", [128, 8], "float32"),
    "c16": ("sbuf", [128, 120], "float32"), "place": ("sbuf", [128, 120], "float32"),
    "win": ("sbuf", [128, 8704], "bfloat16"),
    "xs": ("sbuf", [128, 4096], "float32"), "sb": ("sbuf", [128, 8 * 512], "float32"),
    "rl": ("sbuf", [128, 1024], "float32"),
    "land0": ("sbuf", [128, 4100], "float32"), "land1": ("sbuf", [128, 4100], "float32"),
    "yb": ("sbuf", [128, 3840], "float32"),
    "meta": ("sbuf", [128, 48], "uint16"), "lst": ("sbuf", [128, 5 * 64], "uint16"),
    "cin": ("sbuf", [128, 128], "uint16"),
    "c8": ("sbuf", [128, 16], "float32"), "bp": ("sbuf", [128, 16], "float32"), "w8": ("sbuf", [128, 16], "float32"),
    "th": ("sbuf", [128, 16 * 120], "float16"), "yo": ("sbuf", [128, 240], "float32"),
    "ylst": ("sbuf", [128, 240], "uint16"),
}
for _i in range(8):
    SCRATCH["p%d" % _i] = ("psum", [128, 512], "float32")

SEMAPHORES = ["ex", "x0", "x1", "ones", "nones", "zb0", "zv", "zs", "zc", "c1", "hold", "swr", "dsel", "idb", "idh",
              "zsel", "upn", "va", "vb", "pidx", "c16", "pmod", "pcol", "place", "exb", "ext", "datp", "dat",
              "eqa", "eqb", "cuma", "cumb", "bs", "neg", "qa", "qb", "ma", "mb", "cntp", "cnt", "cself", "posp", "offs",
              "sct", "c8", "bp", "w8", "tha", "thb", "yopa", "yopb", "yoa", "yob", "ylst", "st",
              "sent", "metain", "xin", "rin0", "rin1", "cin", "din0", "din1"]
for _i in range(NB):
    SEMAPHORES += ["lp%d" % _i, "lst%d" % _i]
for _i in range(NU):
    SEMAPHORES += ["gv%d" % _i, "gs%d" % _i]
for _i in range(len(YSTEPS)):
    SEMAPHORES += ["yv%d" % _i, "ys%d" % _i]

COPY = ActivationFunctionType.Copy


def ne(mask):
    return bin(mask).count("1")


def rank_program(g, core, T, topo):
    S, n = T.sem, len(T.cores)
    here = [c for c in T.cores if topo.host(c) == topo.host(core) and topo.chip(c) == topo.chip(core)]
    if not here:
        return
    R = here[0]
    rank = T.rank_of(R)
    chipmates = [c for c in range(R - 8, R + 9) if c >= 0 and c != R and topo.host(c) == topo.host(R)
                 and topo.chip(c) == topo.chip(R)]
    RR = [c for c in chipmates if topo.die(c) == topo.die(R)][:len(R_COUNTS)]
    other = [c for c in chipmates if topo.die(c) != topo.die(R)]
    A, AR = other[0], other[1:len(A_COUNTS)]
    if core != R and core != A and core not in RR and core not in AR:
        return
    rk = lambda o: (rank + o) % n
    far = T.cores[rk(1)]
    off_mask = topo.mask(core, far)
    near_mask = topo.mask(core, R if core != R else A)
    push_mask = near_mask & ~off_mask
    out = [0]

    def send(dst, out_ap, in_ap, sem, mask):
        rid, pid = topo.addr(dst, core)
        g.remote_dma(out_ap, in_ap, S[sem], S.sent, pid, rid, mask)
        out[0] += ne(mask)

    def send_counts(dsts, slot, sem, mask):
        ids = []
        for d in dsts:
            rid, pid = topo.addr(d, core)
            ids.append(DstId(rid=rid, pnc=pid))
        g.remote_dma_fused([RemoteDMATransfer(dst_ids=ids, dma_engine_mask=mask, remote_sem=S[sem],
                                              srcs=[T.meta[:, 32:48]], dsts=[slot] * len(ids))], local_sem=S.sent)
        out[0] += ne(mask)

    land = (T.land0, T.land1)
    cslot = T.cin[:, 16 * rank:16 * rank + 16]
    my_slot = lambda e: land[e][:, SLOT * rank:SLOT * (rank + 1)]

    if core in RR or core in AR:
        onR = core in RR
        me = (RR if onR else AR).index(core)
        counts, units = (R_COUNTS, R_UNITS) if onR else (A_COUNTS, A_UNITS)
        g.wait_ge(S.metain, ne(near_mask) if onR else ne(push_mask))
        send_counts([T.cores[rk(o)] for o in counts[me]], cslot, "cin", off_mask)
        for j, (_, o, e) in enumerate([u for u in units if u[0] == me]):
            g.wait_ge(S["rin%d" % j], ne(push_mask))
            send(T.cores[rk(o)], my_slot(e), T.rl[:, SLOT * j:SLOT * (j + 1)], "din%d" % e, off_mask)
        g.wait_ge(S.sent, out[0])
        return

    isR = core == R
    relays = RR if isR else AR
    units = [(w, rk(o), e) for w, o, e in (R_UNITS if isR else A_UNITS)]
    blocks = []
    for _, d, _ in units:
        if d not in blocks:
            blocks.append(d)
    if isR:
        blocks.append(rank)
    v, s, t, sy = g.vector, g.scalar, g.tensor, g.sync
    winblk = lambda d: T.win[:, BLK * d:BLK * (d + 1)]

    if isR:
        sy.dma_start(T.exi[0:16, :], T.ex[:]).then_inc(S.ex, 16)
        sy.dma_start(T.xs[:, 0:2048], T.x[:, 0:2048]).then_inc(S.x0, 16)
        sy.dma_start(T.xs[:, 2048:4096], T.x[:, 2048:4096]).then_inc(S.x1, 16)

    g.wait_ge(S.ones, 1)
    if isR:
        g.affine_select(T.zsel[0:16, :], T.ones[0:16, 0:240], [[1, 240]], AluOpType.is_equal, 0.0, -112, -1
                        ).then_inc(S.zsel, 1)
        g.iota(T.pidx[:, 0:1], [[0, 1]], 0, 1).then_inc(S.pidx, 1)
    g.affine_select(T.idb[:], T.ones[:, 0:128], [[-1, 128]], AluOpType.is_equal, 0.0, 0, 1).then_inc(S.idb, 1)
    if isR:
        g.iota(T.c16[:], [[16, 120]], 0, 0, allow_small_or_imprecise_dtypes=True).then_inc(S.c16, 1)
    g.iota(T.va[:], [[128, 32], [0, 16]], 0, 0, allow_small_or_imprecise_dtypes=True).then_inc(S.va, 1)
    g.iota(T.vb[:], [[0, 32], [1, 16]], -1, 1, allow_small_or_imprecise_dtypes=True).then_inc(S.vb, 1)
    if isR:
        g.wait_ge(S.nones, 1)
        g.affine_select(T.upn[:], T.nones[:], [[-1, 128]], AluOpType.is_ge, 0.0, 0, 1).then_inc(S.upn, 1)

    v.memset(T.ones[:], 1.0).then_inc(S.ones, 1)
    if isR:
        v.memset(T.nones[:], -1.0).then_inc(S.nones, 1)
    v.memset(winblk(blocks[0]), 0.0).then_inc(S.zb0, 1)
    v.memset(T.swr[:], 0.0).then_inc(S.c1, 1)
    v.memset(T.dsel[:], 0.0).then_inc(S.c1, 1)
    nc1 = 2
    if isR:
        v.memset(T.hold[:], 1.0).then_inc(S.c1, 1)
        nc1 = 3
    v.memset(winblk(blocks[1]), 0.0).then_inc(S.zv, 1)
    v.memset(winblk(blocks[2]), 0.0).then_inc(S.zv, 1)
    v.wait_ge(S.c1, nc1)
    v.memset(T.swr[:, 15::16], 1.0).then_inc(S.swr, 1)
    if isR:
        v.memset(T.hold[:, 0::32], 0.0).then_inc(S.hold, 1)
        for e in range(2):
            v.memset(land[e][:, ZERO:ZERO + 4], 0.0).then_inc(S.zc, 1)
        v.wait_ge(S.pidx, 1)
        v.tensor_scalar(T.pmod[:, 0:1], T.pidx[:, 0:1], 15, None, AluOpType.bitwise_and).then_inc(S.pmod, 1)
    v.wait_ge(S.idb, 1)
    v.tensor_copy(T.dsel[:, 0:128:16], T.idb[:, 0:128:16]).then_inc(S.dsel, 1)
    v.tensor_copy(T.dsel[:, 129:256:16], T.idb[:, 1:128:16]).then_inc(S.dsel, 1)
    if isR:
        v.tensor_copy(T.idh[:], T.idb[:]).then_inc(S.idh, 1)
        v.wait_ge(S.pmod, 1)
        v.tensor_copy(T.pcol[:, 0:1], T.pmod[:, 0:1]).then_inc(S.pcol, 1)
        v.wait_ge(S.ex, 16)
        v.tensor_copy(T.exb[0:16, :], T.exi[0:16, :]).then_inc(S.exb, 1)
        v.wait_ge(S.pcol, 1)
        v.wait_ge(S.c16, 1)
        v.tensor_scalar(T.place[:], T.c16[:], T.pcol[:, 0:1], None, AluOpType.add).then_inc(S.place, 1)

    s.wait_ge(S.zb0, 1)
    nzs = 0
    for d in blocks[3:]:
        s.activation(winblk(d), winblk(blocks[0]), COPY).then_inc(S.zs, 1)
        nzs += 1

    if isR:
        EXT = T.p0[:, 0:32]
        t.wait_ge(S.exb, 1)
        t.wait_ge(S.zsel, 1)
        for h in range(8):
            mm = t.matmul(EXT, T.zsel[0:16, 112 - 16 * h:240 - 16 * h], T.exb[0:16, h::8], h == 0, h == 7)
        mm.then_inc(S.ext, 1)
    t.wait_ge(S.va, 1)
    t.wait_ge(S.vb, 1)
    t.wait_ge(S.dsel, 2)
    t.matmul(T.p4[:], T.dsel[:, 0:128], T.va[:], True, False)
    t.matmul(T.p4[:], T.dsel[:, 128:256], T.vb[:], False, True).then_inc(S.datp, 1)
    s.wait_ge(S.datp, 1)
    s.activation(T.dat[:], T.p4[:], COPY).then_inc(S.dat, 1)
    if isR:
        v.wait_ge(S.ext, 1)
        halves = (("a", 0, T.p1), ("b", 256, T.p6))
        for tag, o, _ in halves:
            for k in range(8):
                v.tensor_scalar(T.eq[:, o + 32 * k:o + 32 * k + 32], EXT, float(o // 32 + k), None, AluOpType.is_equal
                                ).then_inc(S["eq" + tag], 1)
            v.wait_ge(S["eq" + tag], 8)
            if tag == "a":
                v.wait_ge(S.hold, 1)
            v.tensor_tensor_scan(T.cum[:, o:o + 256], T.hold[:, o:o + 256], T.eq[:, o:o + 256], 0.0, AluOpType.mult,
                                 AluOpType.add).then_inc(S["cum" + tag], 1)
        v.tensor_scalar(T.neg[:], EXT, 0.0, None, AluOpType.is_lt).then_inc(S.neg, 1)
        v.tensor_scalar(T.b0[:], EXT, 512.0, None, AluOpType.mult).then_inc(S.bs, 1)
        v.tensor_scalar(T.b1[:], EXT, 0.0, 8704.0, AluOpType.is_lt, AluOpType.mult).then_inc(S.bs, 1)
        v.wait_ge(S.neg, 1)
        v.wait_ge(S.place, 1)
        v.tensor_tensor(T.b2[:], T.neg[:], T.place[:, 0:32], AluOpType.mult).then_inc(S.bs, 1)

        t.wait_ge(S.upn, 1)
        t.wait_ge(S.ones, 1)
        for tag, o, P in halves:
            t.wait_ge(S["cum" + tag], 1)
            t.matmul(P[:, 0:256], T.ones[:, 0:128], T.cum[:, o:o + 256], True, False)
            t.matmul(P[:, 0:256], T.upn[:], T.eq[:, o:o + 256], False, True).then_inc(S["q" + tag], 1)
            v.wait_ge(S["q" + tag], 1)
            v.tensor_tensor(T.mq[:, o:o + 256], P[:, 0:256], T.eq[:, o:o + 256], AluOpType.mult
                            ).then_inc(S["m" + tag], 1)
        t.matmul(T.p2[:, 0:16], T.ones[:, 0:128], T.cum[:, 31::32], True, True).then_inc(S.cntp, 1)
        v.wait_ge(S.cntp, 1)
        v.tensor_copy(T.meta[:, 32:48], T.p2[:, 0:16]).then_inc(S.cnt, 1)
        v.tensor_copy(cslot, T.p2[:, 0:16]).then_inc(S.cself, 1)
        t.wait_ge(S.idh, 1)
        t.wait_ge(S.bs, 3)
        pos = T.p3[:, 0:32]
        for i, b in enumerate((T.b0, T.b1, T.b2)):
            t.matmul(pos, T.idh[:], b[:], i == 0, False)
        for k in range(16):
            if k % 8 == 0:
                t.wait_ge(S["ma" if k == 0 else "mb"], 1)
            mm = t.matmul(pos, T.idh[:], T.mq[:, 32 * k:32 * k + 32], False, k == 15)
        mm.then_inc(S.posp, 1)
        v.wait_ge(S.posp, 1)
        v.tensor_copy(T.meta[:, 0:32], pos).then_inc(S.offs, 1)
        v.wait_ge(S.offs, 1)
    else:
        v.wait_ge(S.metain, ne(near_mask))

    v.wait_ge(S.dat, 1)
    v.wait_ge(S.zb0, 1)
    v.wait_ge(S.zv, 2)
    if nzs:
        v.wait_ge(S.zs, nzs)
    v.tensor_copy(T.win[:].indirect(T.meta[:, 0:32]), T.dat[:]).then_inc(S.sct, 1)
    t.wait_ge(S.swr, 1)
    t.wait_ge(S.sct, 1)
    banks = [T.p5, T.p7, T.p4, T.p0, T.p1]
    for i, d in enumerate(blocks):
        for c in range(16):
            mm = t.matmul(banks[i][:, 0:64], T.swr[:, 15 - c:143 - c], T.win[:, BLK * d + c:BLK * (d + 1):16],
                          c == 0, c == 15)
        mm.then_inc(S["lp%d" % i], 1)
    for q in (v, s):
        if isR:
            q.wait_ge(S.x0, 16)
            q.wait_ge(S.x1, 16)
        else:
            q.wait_ge(S.xin, 2 * ne(near_mask))
    listed = []

    def need_list(d):
        i = blocks.index(d)
        if i not in listed:
            listed.append(i)
            v.wait_ge(S["lp%d" % i], 1)
            v.tensor_copy(T.lst[:, 64 * i:64 * i + 64], banks[i][:, 0:64]).then_inc(S["lst%d" % i], 1)
            for q in (v, s):
                q.wait_ge(S["lst%d" % i], 1)
        return 64 * i

    for u, (_, d, e) in enumerate(units):
        c, o, h = need_list(d) + 32 * e, SLOT * u, SLOT // 2
        v.tensor_copy(T.sb[:, o:o + h], T.xs[:].indirect(T.lst[:, c:c + 16])).then_inc(S["gv%d" % u], 1)
        s.activation(T.sb[:, o + h:o + SLOT], T.xs[:].indirect(T.lst[:, c + 16:c + 32]), COPY
                     ).then_inc(S["gs%d" % u], 1)
    if isR:
        c, u = need_list(rank), len(units)
        v.tensor_copy(my_slot(0), T.xs[:].indirect(T.lst[:, c:c + 32])).then_inc(S["gv%d" % u], 1)
        s.activation(my_slot(1), T.xs[:].indirect(T.lst[:, c + 32:c + 64]), COPY).then_inc(S["gs%d" % u], 1)

    if isR:
        g.wait_ge(S.x0, 16)
        send(A, T.xs[:, 0:2048], T.xs[:, 0:2048], "xin", near_mask)
        g.wait_ge(S.cnt, 1)
        send_counts(RR, T.meta[:, 32:48], "metain", near_mask)
        g.wait_ge(S.offs, 1)
        send(A, T.meta[:], T.meta[:], "metain", near_mask)
        g.wait_ge(S.x1, 16)
        send(A, T.xs[:, 2048:4096], T.xs[:, 2048:4096], "xin", near_mask)
    else:
        g.wait_ge(S.metain, ne(near_mask))
        send_counts([T.cores[rk(o)] for o in A_COUNTS["d"]], cslot, "cin", off_mask)
        send_counts(AR, T.meta[:, 32:48], "metain", push_mask)
    pushed = [0] * len(relays)
    for u, (w, d, e) in enumerate(units):
        g.wait_ge(S["gv%d" % u], 1)
        g.wait_ge(S["gs%d" % u], 1)
        src = T.sb[:, SLOT * u:SLOT * (u + 1)]
        if w == "d":
            send(T.cores[d], my_slot(e), src, "din%d" % e, off_mask)
        else:
            j = pushed[w]
            pushed[w] += 1
            send(relays[w], T.rl[:, SLOT * j:SLOT * (j + 1)], src, "rin%d" % j, push_mask)
    g.wait_ge(S.sent, out[0])
    if not isR:
        return

    v.wait_ge(S.cself, 1)
    v.wait_ge(S.cin, (n - 1) * ne(off_mask))
    for e in range(2):
        v.tensor_copy(T.c8[:, 8 * e:8 * e + 8], T.cin[:, 2 * rank + e::16]).then_inc(S.c8, 1)
    v.wait_ge(S.c8, 2)
    for e in range(2):
        c = T.c8[:, 8 * e:8 * e + 8]
        v.tensor_tensor_scan(T.bp[:, 8 * e:8 * e + 8], T.ones[:, 0:8], c, 0.0, AluOpType.mult, AluOpType.add
                             ).then_inc(S.bp, 1)
        v.tensor_scalar(T.w8[:, 8 * e:8 * e + 8], c, -1.0, float(SLOT), AluOpType.mult, AluOpType.add
                        ).then_inc(S.w8, 1)
    v.wait_ge(S.bp, 2)
    v.wait_ge(S.w8, 2)
    for e, tag, P in ((0, "a", T.p3), (1, "b", T.p6)):
        for r in range(n):
            j = 8 * e + r
            v.tensor_scalar(T.th[:, 120 * j:120 * j + 120], T.place[:], T.bp[:, j:j + 1], T.w8[:, j:j + 1],
                            AluOpType.is_ge, AluOpType.mult).then_inc(S["th" + tag], 1)
        t.wait_ge(S["th" + tag], n)
        for r in range(n):
            j = 8 * e + r
            mm = t.matmul(P[:, 0:120], T.idh[:], T.th[:, 120 * j:120 * j + 120], r == 0, r == n - 1)
        mm.then_inc(S["yop" + tag], 1)
    for e, tag, P in ((0, "a", T.p3), (1, "b", T.p6)):
        o = T.yo[:, 120 * e:120 * e + 120]
        v.wait_ge(S["yop" + tag], 1)
        v.tensor_tensor(o, P[:, 0:120], T.place[:], AluOpType.add).then_inc(S["yo" + tag], 1)
        v.wait_ge(S["yo" + tag], 1)
        v.tensor_scalar(T.ylst[:, 120 * e:120 * e + 120], o, float(ZERO), None, AluOpType.min).then_inc(S.ylst, 1)

    last = len(units)
    for q in (v, s):
        q.wait_ge(S.ylst, 2)
        q.wait_ge(S.zc, 2)
        q.wait_ge(S["gv%d" % last], 1)
        q.wait_ge(S["gs%d" % last], 1)
    o = 0
    for i, (e, w) in enumerate(YSTEPS):
        if i == 0 or YSTEPS[i - 1][0] != e:
            for q in (v, s):
                q.wait_ge(S["din%d" % e], (n - 1) * ne(off_mask))
        m = o + w // 2
        W = land[e][:, 0:ZERO + 1]
        v.tensor_copy(T.yb[:, o:m], W.indirect(T.ylst[:, o // 16:m // 16])).then_inc(S["yv%d" % i], 1)
        s.activation(T.yb[:, m:o + w], W.indirect(T.ylst[:, m // 16:(o + w) // 16]), COPY).then_inc(S["ys%d" % i], 1)
        sy.wait_ge(S["yv%d" % i], 1)
        sy.wait_ge(S["ys%d" % i], 1)
        sy.dma_start(T.y[:, o:o + w], T.yb[:, o:o + w]).then_inc(S.st, 16)
        o += w
    sy.wait_ge(S.st, 16 * len(YSTEPS))
